import numpy as np
import ml_dtypes


def mxq(x, axis, fmt="e4m3"):
    dtype, down = {"e4m3": (ml_dtypes.float8_e4m3fn, 7), "e5m2": (ml_dtypes.float8_e5m2, 14)}[fmt]
    v = np.moveaxis(np.asarray(x, np.float32).astype(ml_dtypes.bfloat16).astype(np.float64), axis, -1)
    blocks = v.reshape(v.shape[:-1] + (-1, 32))
    amax = np.abs(blocks).max(-1, keepdims=True)
    byte = np.maximum(np.where(amax > 0, np.frexp(amax)[1] - 1 + 127, 0) - down, 1)
    scale = np.exp2(byte - 127.0)
    codes = (blocks / scale).astype(np.float32).astype(dtype).astype(np.float64)
    return np.moveaxis((codes * scale).reshape(v.shape), -1, axis)


WIDE = False


def mx_kscale(k):
    if not WIDE:
        return np.ones(k)
    levels = np.array([10, -10, 5, -5, 0])
    if k % 512:
        return np.exp2(np.random.permutation(np.resize(levels, k // 32))).repeat(32)
    a = np.empty((k // 512, 16))
    for p in range(k // 512):
        a[p, :8] = np.random.permutation(np.resize(levels, 8))
        for g in range(8):
            far = levels[np.abs(levels - a[p, g]) >= 10]
            a[p, g + 8] = far[np.random.randint(len(far))]
    return np.exp2(a.ravel()).repeat(32)


def f64(x):
    return np.asarray(x).astype(np.float64)


def striped(idx):
    return np.tile(idx.reshape(-1, 16).T, (8, 1)).astype(np.uint16)


def unstriped(offs):
    return offs[:16].T.reshape(-1).astype(np.int64)


def pack_weight(w):
    k, n = w.shape
    w = f64(np.asarray(w, np.float32).astype(ml_dtypes.bfloat16)).reshape(k // 32, 32, n)
    amax = np.abs(w).max(1)
    byte = np.clip(np.where(amax > 0, np.frexp(amax)[1] - 1 + 127 - 7, 1), 1, 254)
    scaled = (w * np.exp2(127.0 - byte)[:, None, :]).reshape(k, n).astype(np.float32)
    words = np.ascontiguousarray(scaled.reshape(k // 512, 128, 4, n).transpose(0, 1, 3, 2)).astype(ml_dtypes.float8_e4m3fn).view(np.uint8)
    return words, np.ascontiguousarray(byte.astype(np.uint8).reshape(k // 512, 16, n))


def unpack_weight(words, scales):
    g, p, n, _ = words.shape
    vals = np.ascontiguousarray(words).view(ml_dtypes.float8_e4m3fn).astype(np.float64) * np.repeat(np.exp2(scales.astype(np.float64) - 127.0), 8, axis=1)[..., None]
    return vals.transpose(0, 1, 3, 2).reshape(g * 512, n)


E2M1 = np.array([0.0, 0.5, 1.0, 1.5, 2.0, 3.0, 4.0, 6.0, -0.0, -0.5, -1.0, -1.5, -2.0, -3.0, -4.0, -6.0])


def pack_fp4(w):
    k, n = w.shape
    w = f64(np.asarray(w, np.float32).astype(ml_dtypes.bfloat16)).reshape(k // 32, 32, n)
    amax = np.abs(w).max(1)
    mant, ex = np.frexp(amax / 6.0)
    byte = np.clip(np.where(amax > 0, np.where(mant > 0.5, ex, ex - 1) + 127, 1), 1, 254)
    scaled = (w * np.exp2(127.0 - byte)[:, None, :]).reshape(k, n).astype(np.float32)
    c = np.ascontiguousarray(scaled.reshape(k // 512, 128, 4, n).transpose(0, 1, 3, 2)).astype(ml_dtypes.float4_e2m1fn).view(np.uint8) & 0xF
    words = (c[..., 0::2] | (c[..., 1::2] << 4)).reshape(k // 512, 128, 2 * n)
    return np.ascontiguousarray(words), np.ascontiguousarray(byte.astype(np.uint8).reshape(k // 512, 16, n))


def unpack_fp4(words, scales):
    g, _, n = scales.shape
    words = np.ascontiguousarray(words).reshape(g, 128, n, 2)
    nib = np.empty((g, 128, n, 4), np.uint8)
    nib[..., 0::2] = words & 0xF
    nib[..., 1::2] = words >> 4
    vals = E2M1[nib] * np.repeat(np.exp2(scales.astype(np.float64) - 127.0), 8, axis=1)[..., None]
    return vals.transpose(0, 1, 3, 2).reshape(g * 512, n)


def planes(y):
    n, m = y.shape
    v = y.astype(np.float32).astype(ml_dtypes.bfloat16).astype(np.float64).reshape(n // 32, 32, m)
    top = np.abs(v).max(1)
    byte = np.clip(np.where(top > 0, np.frexp(top)[1] - 1 + 127 - 7, 1), 1, 254)
    codes = (v * np.exp2(127.0 - byte)[:, None, :]).reshape(n, m).astype(np.float32).astype(ml_dtypes.float8_e4m3fn).view(np.uint8)
    words = codes.reshape(n // 512, 128, 4, m).transpose(0, 1, 3, 2)
    return np.ascontiguousarray(words), np.ascontiguousarray(byte.astype(np.uint8).reshape(n // 512, 16, m))


def sigmoid(v):
    return 1.0 / (1.0 + np.exp(-np.maximum(v, -700.0)))


def gelu(v):
    return 0.5 * v * (1.0 + np.tanh(np.sqrt(2.0 / np.pi) * (v + 0.044715 * v**3)))


K, T, S, H, Z, W = 512, 1024, 512, 512, 512, 2048
P = 2 ** 7


def setup_inputs():
    n = np.random.standard_normal
    s = mx_kscale(K)[:, None]
    u = mx_kscale(H)
    packed_xT = pack_weight(n((K, T)) * s)
    packed_w1 = pack_fp4(n((K, H)) / np.sqrt(K) / s)
    packed_eT = pack_weight(n((K, W)) * s)
    packed_w2 = pack_fp4(n((K, H)) / np.sqrt(K) / s)
    packed_w3 = pack_fp4(n((K, H)) / np.sqrt(K) / s)
    return {
        "x_words": packed_xT[0],
        "x_scales": packed_xT[1],
        "w1_words": packed_w1[0],
        "w1_scales": packed_w1[1],
        "e_words": packed_eT[0],
        "e_scales": packed_eT[1],
        "w2_words": packed_w2[0],
        "w2_scales": packed_w2[1],
        "w3_words": packed_w3[0],
        "w3_scales": packed_w3[1],
        "unit": (np.random.uniform(0.6, 1.4, (H, 1)) * u[:, None]).astype(np.float32),
        "unit2": (np.random.uniform(0.6, 1.4, (H, 1)) / np.sqrt(H) / u[:, None]).astype(np.float32),
        "abd": (np.tile(np.random.uniform(0.2, 1.5, W), (P, 1))).astype(np.float32),
        "offs": striped(np.random.permutation(T)[:S]),
        "pry": striped(np.random.permutation(W)[:Z]),
        "ref": striped(np.random.permutation(Z)),
        "sw": striped(np.random.permutation(Z)),
    }


def reference(x_words, x_scales, w1_words, w1_scales, e_words, e_scales, w2_words, w2_scales, w3_words, w3_scales, unit, unit2, abd, offs, pry, ref, sw):
    xq = unpack_weight(x_words, x_scales)[:, unstriped(offs)]
    y = unpack_fp4(w1_words, w1_scales).T @ xq
    att = gelu(y)
    hid = f64(unit) * att
    e_pry = unpack_weight(e_words, e_scales)[:, unstriped(pry)]
    ye = unpack_fp4(w2_words, w2_scales).T @ e_pry
    yg = unpack_fp4(w3_words, w3_scales).T @ e_pry
    gr = yg[:, unstriped(ref)]
    vul = ye * (-0.7 * sigmoid(gr) + 1.2)
    hid2 = f64(unit2) * vul
    sc = mxq(hid, 0, "e4m3").T @ mxq(hid2, 0, "e4m3")
    rate = (np.exp(1.2 * np.tanh(sc))) * (f64(abd)[:1][:, unstriped(pry)])
    tot = rate.mean(axis=1, keepdims=True)
    feed = rate / (tot + 0.5)
    fsw = feed[:, unstriped(sw)] + 0.5
    rel = (f64(abd)[:1][:, unstriped(pry)]) / fsw
    out_0 = feed * rel
    return (out_0,) + planes(out_0)

@@ -1,0 +1,269 @@
+from contextlib import ExitStack
+
+import concourse.mybir as mybir
+from concourse.masks import make_identity
+
+F32 = mybir.dt.float32
+BF16 = mybir.dt.bfloat16
+I32 = mybir.dt.int32
+U32 = mybir.dt.uint32
+U16 = mybir.dt.uint16
+U8 = mybir.dt.uint8
+FP8X4 = mybir.dt.float8_e4m3fn_x4
+FP4X4 = mybir.dt.float4_e2m1fn_x4
+ALU = mybir.AluOpType
+ACT = mybir.ActivationFunctionType
+
+P = 128
+N = 512
+HALF = N // 2
+FLOPS = 4 * 2 * N * N * N
+
+
+def tile_picked_yfoodwb_rel_po_kernel(
+    tc, x_words, x_scales, w1_words, w1_scales, e_words, e_scales, w2_words, w2_scales,
+    w3_words, w3_scales, unit, unit2, abd, offs, pry, ref, sw, out_0, out_1, out_2,
+):
+    nc = tc.nc
+    n_x = x_scales.shape[2]
+    n_e = e_scales.shape[2]
+
+    with ExitStack() as ctx:
+        sb = ctx.enter_context(tc.tile_pool(name="sb", bufs=1))
+        psum = ctx.enter_context(tc.psum_pool(name="psum", bufs=1))
+
+        def sbuf(name, shape, dtype, tag=""):
+            return sb.tile(shape, dtype, name=name, tag=tag, align_bytes=64)
+
+        def bank(i, name):
+            return psum.tile([P, N], F32, name=name, tag="bank%d" % i)
+
+        def load_list(name, src):
+            t = sbuf(name, [P, N // 16], U16)
+            nc.sync.dma_start(t[:], src)
+            return t
+
+        def load_words(queue, name, src):
+            t = sbuf(name, [P, src.shape[1] // 4], I32, tag=name)
+            queue.dma_start(t[:], src.bitcast(I32))
+            return t
+
+        def scale_tile(engine, name, width):
+            t = sbuf(name, [P, width], U8, tag=name)
+            engine.memset(t[:].bitcast(I32), 0)
+            return t
+
+        def load_scales(queue, t, src, quadrants=range(4)):
+            for q in quadrants:
+                queue.dma_start(t[32 * q : 32 * q + 4, :].bitcast(I32), src[0, 4 * q : 4 * q + 4, :].bitcast(I32))
+
+        def deal(name, words, scales):
+            dw = sbuf(name + "_words", [P, 2 * N], U8)
+            ds = sbuf(name + "_scales", [P, N], U8)
+            nc.vector.tensor_copy(
+                dw[:].bitcast(I32).rearrange("p (r b c) -> p b r c", r=4, c=4),
+                words[:].rearrange("p (b r c) -> p b r c", r=4, c=4),
+            )
+            nc.vector.tensor_copy(
+                ds[:].bitcast(I32).rearrange("p (r b c) -> p b r c", r=4, c=2),
+                scales[:].bitcast(I32).rearrange("p (b r c) -> p b r c", r=4, c=2),
+            )
+            return dw, ds
+
+        def weight_pass(out, w, r, codes, scales, cols):
+            nc.tensor.matmul_mx(
+                out=out,
+                lhsT=w[0][:, 2 * P * r : 2 * P * (r + 1)].bitcast(FP4X4),
+                lhsT_scale=w[1][:, P * r : P * (r + 1)],
+                rhs=codes[:, cols].bitcast(FP8X4),
+                rhs_scale=scales[:, cols],
+                start=True,
+                stop=True,
+            )
+
+        def half_list(t, h):
+            return t[:, 16 * h : 16 * (h + 1)]
+
+        xs_raw = scale_tile(nc.vector, "xs_raw", n_x)
+        w1s_raw = scale_tile(nc.vector, "w1s_raw", N)
+        es_raw = scale_tile(nc.vector, "es_raw", n_e)
+        w3s_raw = scale_tile(nc.vector, "w3s_raw", N)
+        w2s_raw = scale_tile(nc.vector, "w2s_raw", N)
+        w1w_raw = load_words(nc.gpsimd, "w1w_raw", w1_words[0])
+        unit_rows = sbuf("unit_rows", [P, P], F32)
+        nc.gpsimd.memset(unit_rows[:], 0.0)
+        for j, u in enumerate((unit, unit2)):
+            nc.gpsimd.dma_start(
+                unit_rows[4 * j : 4 * j + 4, :].rearrange("r (b q) -> r b q", q=8),
+                u.rearrange("(b r q) o -> r b (q o)", r=4, q=8),
+            )
+        ident = sbuf("ident", [P, P], F32)
+        make_identity(nc, ident[:])
+        load_scales(nc.gpsimd, w2s_raw, w2_scales, range(2, 4))
+
+        offs_t = load_list("offs_t", offs)
+        xw_raw = load_words(nc.sync, "xw_raw", x_words[0].rearrange("p n t -> p (n t)"))
+        load_scales(nc.sync, xs_raw, x_scales)
+        pry_t = load_list("pry_t", pry)
+        load_scales(nc.sync, es_raw, e_scales, range(1))
+        ew_raw = load_words(nc.sync, "ew_raw", e_words[0].rearrange("p n t -> p (n t)"))
+        load_scales(nc.sync, w1s_raw, w1_scales)
+        load_scales(nc.sync, es_raw, e_scales, range(1, 4))
+        w3w_raw = load_words(nc.sync, "w3w_raw", w3_words[0])
+        load_scales(nc.sync, w3s_raw, w3_scales)
+        w2w_raw = load_words(nc.sync, "w2w_raw", w2_words[0])
+        ref_t = load_list("ref_t", ref)
+        load_scales(nc.sync, w2s_raw, w2_scales, range(2))
+        abd_t = sbuf("abd_t", [P, n_e], F32)
+        nc.sync.dma_start(abd_t[:], abd)
+        sw_t = load_list("sw_t", sw)
+
+        xw = sbuf("xw", [P, N], U32)
+        xs = sbuf("xs", [P, N], U8)
+        nc.vector.tensor_copy(xw[:], xw_raw[:].bitcast(U32).indirect(offs_t[:]))
+        nc.vector.tensor_copy(xs[:], xs_raw[:].indirect(offs_t[:]))
+        w1 = deal("w1", w1w_raw, w1s_raw)
+        ew = sbuf("ew", [P, N], U32, tag="w1s_raw")
+        es = sbuf("es", [P, N], U8)
+        nc.vector.tensor_copy(ew[:], ew_raw[:].bitcast(U32).indirect(pry_t[:]))
+        nc.vector.tensor_copy(es[:], es_raw[:].indirect(pry_t[:]))
+        w3 = deal("w3", w3w_raw, w3s_raw)
+        w2 = deal("w2", w2w_raw, w2s_raw)
+
+        att = sbuf("att", [P, 4, 4, 32, 4], F32)
+        for b in range(4):
+            y = bank(b, "y%d" % b)
+            for r in range(4):
+                weight_pass(y[:, P * r : P * (r + 1)], w1, r, xw, xs, slice(P * b, P * (b + 1)))
+            nc.scalar.activation(
+                att[:, :, b, :, :].rearrange("p s m r -> p m s r"),
+                y[:].rearrange("p (r m s) -> p m s r", r=4, s=4),
+                ACT.Gelu_apprx_tanh,
+            )
+        units_ps = bank(7, "units_ps")
+        nc.tensor.transpose(units_ps[:, 0:P], unit_rows[:], ident[:])
+        units = sbuf("units", [P, 8], F32)
+        nc.vector.tensor_copy(units[:], units_ps[:, 0:8])
+
+        th = []
+        for r in range(4):
+            yg = bank(4 + r, "yg%d" % r)
+            weight_pass(yg[:], w3, r, ew, es, slice(0, N))
+            t = sbuf("th%d" % r, [P, N], F32)
+            nc.scalar.activation(t[:], yg[:], ACT.Tanh, scale=0.5)
+            th.append(t)
+        ye = {}
+        for h in range(2):
+            for pair in range(2):
+                t = bank(2 * h + pair, "ye%d_%d" % (h, pair))
+                for j in range(2):
+                    ye[h, 2 * pair + j] = t[:, HALF * j : HALF * (j + 1)]
+                    weight_pass(ye[h, 2 * pair + j], w2, 2 * pair + j, ew, es, slice(HALF * h, HALF * (h + 1)))
+
+        hid = sbuf("hid", [P, N, 4], BF16, tag="w3s_raw")
+        nc.vector.tensor_tensor(
+            hid[:],
+            att[:].rearrange("p s b m r -> p (s b m) r"),
+            units[:, 0:4].rearrange("p (o r) -> p o r", o=1).to_broadcast([P, N, 4]),
+            ALU.mult,
+        )
+        hid_codes = sbuf("hid_codes", [P, N], U32)
+        hid_scales = sbuf("hid_scales", [P, N], U8)
+        nc.vector.quantize_mx(out=hid_codes[:].bitcast(FP8X4), scales=hid_scales[:], in_=hid[:].rearrange("p n r -> p (n r)"))
+
+        scores = {}
+        rate = sbuf("rate", [P, 4, N], F32)
+        top = sbuf("top", [P, 4, N], F32)
+        sums = sbuf("sums", [P, 4, 2], F32)
+        for h in range(2):
+            cols = slice(HALF * h, HALF * (h + 1))
+            planes = sbuf("planes%d" % h, [P, 4, HALF], BF16, tag="planes")
+            for r in range(4):
+                gate = sbuf("gate%d_%d" % (h, r), [P, HALF], F32)
+                nc.scalar.activation(gate[:], th[r][:].indirect(half_list(ref_t, h)), ACT.Copy, scale=-0.35, bias=0.85)
+                nc.vector.scalar_tensor_tensor(planes[:, r, :], ye[h, r], units[:, 4 + r : 5 + r], gate[:], ALU.mult, ALU.mult)
+            hid2 = sbuf("hid2_%d" % h, [P, HALF, 4], BF16, tag="hid2_%d" % h)
+            nc.vector.tensor_copy(hid2[:], planes[:].rearrange("p r n -> p n r"))
+            codes = sbuf("hid2_codes%d" % h, [P, HALF], U32)
+            scales = sbuf("hid2_scales%d" % h, [P, HALF], U8)
+            nc.vector.quantize_mx(out=codes[:].bitcast(FP8X4), scales=scales[:], in_=hid2[:].rearrange("p n r -> p (n r)"))
+            for pair in range(2):
+                sc = bank(4 + 2 * h + pair, "sc%d_%d" % (h, pair))
+                for j in range(2):
+                    s = 2 * pair + j
+                    nc.tensor.matmul_mx(
+                        out=sc[:, HALF * j : HALF * (j + 1)],
+                        lhsT=hid_codes[:, P * s : P * (s + 1)].bitcast(FP8X4),
+                        lhsT_scale=hid_scales[:, P * s : P * (s + 1)],
+                        rhs=codes[:].bitcast(FP8X4),
+                        rhs_scale=scales[:],
+                        start=True,
+                        stop=True,
+                    )
+                scores[h, pair] = sc
+
+        prey = sbuf("prey", [P, N], F32, tag="hid2_1")
+        nc.vector.tensor_copy(prey[:], abd_t[:].indirect(pry_t[:]))
+        prey_sq = sbuf("prey_sq", [P, N], F32)
+        nc.vector.scalar_tensor_tensor(prey_sq[:], prey[:], 2.0, prey[:], ALU.mult, ALU.mult)
+
+        for h in range(2):
+            cols = slice(HALF * h, HALF * (h + 1))
+            for pair in range(2):
+                bounded = sbuf("bounded%d_%d" % (h, pair), [P, N], F32)
+                nc.scalar.activation(bounded[:], scores[h, pair][:], ACT.Tanh)
+                growth = sbuf("growth%d_%d" % (h, pair), [P, 2, HALF], F32)
+                nc.scalar.activation(growth[:].rearrange("p j n -> p (j n)"), bounded[:], ACT.Exp, scale=1.2)
+                for j in range(2):
+                    s = 2 * pair + j
+                    nc.vector.scalar_tensor_tensor(
+                        rate[:, s, cols], growth[:, j, :], 1.0, prey[:, cols], ALU.mult, ALU.mult, accum_out=sums[:, s, h : h + 1]
+                    )
+                nc.vector.tensor_tensor(
+                    top[:, 2 * pair : 2 * pair + 2, cols],
+                    growth[:],
+                    prey_sq[:, cols].rearrange("p (o n) -> p o n", o=1).to_broadcast([P, 2, HALF]),
+                    ALU.mult,
+                )
+
+        total = sbuf("total", [P, 4], F32)
+        shift = sbuf("shift", [P, 4], F32)
+        for pair in range(2):
+            two = slice(2 * pair, 2 * pair + 2)
+            nc.vector.tensor_tensor(total[:, two], sums[:, two, 0], sums[:, two, 1], ALU.add)
+            nc.vector.tensor_scalar(shift[:, two], total[:, two], 0.5 / N, 0.25, ALU.mult, ALU.add)
+
+        inverse = []
+        for s in range(4):
+            positive = sbuf("positive%d" % s, [P, N], F32)
+            nc.vector.tensor_scalar(positive[:], rate[:, s, :], shift[:, s : s + 1], 0.0, ALU.add, ALU.is_gt)
+            root = sbuf("root%d" % s, [P, N], F32)
+            nc.scalar.activation(root[:], rate[:, s, :], ACT.Abs_reciprocal_sqrt, bias=shift[:, s : s + 1])
+            size = sbuf("size%d" % s, [P, N], F32, tag="size%d" % s)
+            nc.scalar.activation(size[:], root[:], ACT.Square)
+            inv = sbuf("inverse%d" % s, [P, N], F32)
+            nc.vector.scalar_tensor_tensor(inv[:], positive[:], 0.5, size[:], ALU.subtract, ALU.mult)
+            inverse.append(inv)
+
+        out_rows = out_0.rearrange("(p s) e -> p s e", s=4)
+        out_words = out_1[0].rearrange("p n t -> p (n t)").bitcast(I32)
+        out_scales = sbuf("out_scales", [P, N], U8)
+        for h in range(2):
+            cols = slice(HALF * h, HALF * (h + 1))
+            result = sbuf("result%d" % h, [P, 4, HALF], F32, tag="size3" if h else "result0")
+            for s in range(4):
+                nc.vector.tensor_tensor(result[:, s, :], inverse[s][:].indirect(half_list(sw_t, h)), top[:, s, cols], ALU.mult)
+            nc.sync.dma_start(out_rows[:, :, cols], result[:])
+            rounded = sbuf("rounded%d" % h, [P, HALF, 4], BF16)
+            turned = result[:].rearrange("p s n -> p n s")
+            if h == 0:
+                nc.scalar.copy(rounded[:], turned)
+            else:
+                nc.scalar.copy(rounded[:, 0:96, :], turned[:, 0:96, :])
+                nc.vector.tensor_copy(rounded[:, 96:HALF, :], turned[:, 96:HALF, :])
+            out_codes = sbuf("out_codes%d" % h, [P, HALF], U32)
+            nc.vector.quantize_mx(out=out_codes[:].bitcast(FP8X4), scales=out_scales[:, cols], in_=rounded[:].rearrange("p n s -> p (n s)"))
+            nc.sync.dma_start(out_words[:, cols], out_codes[:].bitcast(I32))
+        for q in range(4):
+            queue = nc.scalar if q % 2 else nc.sync
+            queue.dma_start(out_2[0, 4 * q : 4 * q + 4, :].bitcast(I32), out_scales[32 * q : 32 * q + 4, :].bitcast(I32))

@@ -99,7 +99,6 @@ def tile_picked_yfoodwb_rel_po_kernel(
             )
         ident = sbuf("ident", [P, P], F32)
         make_identity(nc, ident[:])
-        load_scales(nc.gpsimd, w2s_raw, w2_scales, range(2, 4))
 
         offs_t = load_list("offs_t", offs)
         xw_raw = load_words(nc.sync, "xw_raw", x_words[0].rearrange("p n t -> p (n t)"))
@@ -113,7 +112,7 @@ def tile_picked_yfoodwb_rel_po_kernel(
         load_scales(nc.sync, w3s_raw, w3_scales)
         w2w_raw = load_words(nc.sync, "w2w_raw", w2_words[0])
         ref_t = load_list("ref_t", ref)
-        load_scales(nc.sync, w2s_raw, w2_scales, range(2))
+        load_scales(nc.sync, w2s_raw, w2_scales)
         abd_t = sbuf("abd_t", [P, n_e], F32)
         nc.sync.dma_start(abd_t[:], abd)
         sw_t = load_list("sw_t", sw)
@@ -140,7 +139,7 @@ def tile_picked_yfoodwb_rel_po_kernel(
                 y[:].rearrange("p (r m s) -> p m s r", r=4, s=4),
                 ACT.Gelu_apprx_tanh,
             )
-        units_ps = bank(7, "units_ps")
+        units_ps = bank(0, "units_ps")
         nc.tensor.transpose(units_ps[:, 0:P], unit_rows[:], ident[:])
         units = sbuf("units", [P, 8], F32)
         nc.vector.tensor_copy(units[:], units_ps[:, 0:8])
@@ -172,7 +171,6 @@ def tile_picked_yfoodwb_rel_po_kernel(
         nc.vector.quantize_mx(out=hid_codes[:].bitcast(FP8X4), scales=hid_scales[:], in_=hid[:].rearrange("p n r -> p (n r)"))
 
         scores = {}
-        rate = sbuf("rate", [P, 4, N], F32)
         top = sbuf("top", [P, 4, N], F32)
         sums = sbuf("sums", [P, 4, 2], F32)
         for h in range(2):
@@ -202,10 +200,9 @@ def tile_picked_yfoodwb_rel_po_kernel(
                     )
                 scores[h, pair] = sc
 
-        prey = sbuf("prey", [P, N], F32, tag="hid2_1")
-        nc.vector.tensor_copy(prey[:], abd_t[:].indirect(pry_t[:]))
-        prey_sq = sbuf("prey_sq", [P, N], F32)
-        nc.vector.scalar_tensor_tensor(prey_sq[:], prey[:], 2.0, prey[:], ALU.mult, ALU.mult)
+        prey = sbuf("prey", [P, N], F32)
+        nc.scalar.activation(prey[:], abd_t[:].indirect(pry_t[:]), ACT.Copy)
+        rate = sbuf("rate", [P, 4, N], F32, tag="hid2_1")
 
         for h in range(2):
             cols = slice(HALF * h, HALF * (h + 1))
@@ -219,12 +216,6 @@ def tile_picked_yfoodwb_rel_po_kernel(
                     nc.vector.scalar_tensor_tensor(
                         rate[:, s, cols], growth[:, j, :], 1.0, prey[:, cols], ALU.mult, ALU.mult, accum_out=sums[:, s, h : h + 1]
                     )
-                nc.vector.tensor_tensor(
-                    top[:, 2 * pair : 2 * pair + 2, cols],
-                    growth[:],
-                    prey_sq[:, cols].rearrange("p (o n) -> p o n", o=1).to_broadcast([P, 2, HALF]),
-                    ALU.mult,
-                )
 
         total = sbuf("total", [P, 4], F32)
         shift = sbuf("shift", [P, 4], F32)
@@ -235,14 +226,15 @@ def tile_picked_yfoodwb_rel_po_kernel(
 
         inverse = []
         for s in range(4):
-            positive = sbuf("positive%d" % s, [P, N], F32)
-            nc.vector.tensor_scalar(positive[:], rate[:, s, :], shift[:, s : s + 1], 0.0, ALU.add, ALU.is_gt)
+            nc.vector.tensor_tensor(top[:, s, :], rate[:, s, :], prey[:], ALU.mult)
             root = sbuf("root%d" % s, [P, N], F32)
             nc.scalar.activation(root[:], rate[:, s, :], ACT.Abs_reciprocal_sqrt, bias=shift[:, s : s + 1])
-            size = sbuf("size%d" % s, [P, N], F32, tag="size%d" % s)
+            size = sbuf("size%d" % s, [P, N], F32)
             nc.scalar.activation(size[:], root[:], ACT.Square)
+            sign = sbuf("sign%d" % s, [P, N], F32)
+            nc.scalar.activation(sign[:], rate[:, s, :], ACT.Sign, bias=shift[:, s : s + 1])
             inv = sbuf("inverse%d" % s, [P, N], F32)
-            nc.vector.scalar_tensor_tensor(inv[:], positive[:], 0.5, size[:], ALU.subtract, ALU.mult)
+            nc.vector.tensor_tensor(inv[:], sign[:], size[:], ALU.mult)
             inverse.append(inv)
 
         out_rows = out_0.rearrange("(p s) e -> p s e", s=4)
@@ -250,7 +242,7 @@ def tile_picked_yfoodwb_rel_po_kernel(
         out_scales = sbuf("out_scales", [P, N], U8)
         for h in range(2):
             cols = slice(HALF * h, HALF * (h + 1))
-            result = sbuf("result%d" % h, [P, 4, HALF], F32, tag="size3" if h else "result0")
+            result = sbuf("result%d" % h, [P, 4, HALF], F32)
             for s in range(4):
                 nc.vector.tensor_tensor(result[:, s, :], inverse[s][:].indirect(half_list(sw_t, h)), top[:, s, cols], ALU.mult)
             nc.sync.dma_start(out_rows[:, :, cols], result[:])
@@ -259,8 +251,7 @@ def tile_picked_yfoodwb_rel_po_kernel(
             if h == 0:
                 nc.scalar.copy(rounded[:], turned)
             else:
-                nc.scalar.copy(rounded[:, 0:96, :], turned[:, 0:96, :])
-                nc.vector.tensor_copy(rounded[:, 96:HALF, :], turned[:, 96:HALF, :])
+                nc.vector.tensor_copy(rounded[:], turned)
             out_codes = sbuf("out_codes%d" % h, [P, HALF], U32)
             nc.vector.quantize_mx(out=out_codes[:].bitcast(FP8X4), scales=out_scales[:, cols], in_=rounded[:].rearrange("p n s -> p (n s)"))
             nc.sync.dma_start(out_words[:, cols], out_codes[:].bitcast(I32))

@@ -1,3 +1,4 @@
+import math
 from contextlib import ExitStack
 
 import concourse.mybir as mybir
@@ -19,14 +20,19 @@ N = 512
 HALF = N // 2
 FLOPS = 4 * 2 * N * N * N
 
+GATE_SLOPE, GATE_LEVEL = -0.35, 0.85
+VECTOR_GATE = (0, 3)
+SCALAR_SLOTS = 2
+SCALAR_COLUMNS = 96
+
 
 def tile_picked_yfoodwb_rel_po_kernel(
     tc, x_words, x_scales, w1_words, w1_scales, e_words, e_scales, w2_words, w2_scales,
     w3_words, w3_scales, unit, unit2, abd, offs, pry, ref, sw, out_0, out_1, out_2,
 ):
     nc = tc.nc
-    n_x = x_scales.shape[2]
-    n_e = e_scales.shape[2]
+    predators = x_scales.shape[2]
+    all_prey = e_scales.shape[2]
 
     with ExitStack() as ctx:
         sb = ctx.enter_context(tc.tile_pool(name="sb", bufs=1))
@@ -38,6 +44,12 @@ def tile_picked_yfoodwb_rel_po_kernel(
         def bank(i, name):
             return psum.tile([P, N], F32, name=name, tag="bank%d" % i)
 
+        def half(h):
+            return slice(HALF * h, HALF * (h + 1))
+
+        def half_list(t, h):
+            return t[:, 16 * h : 16 * (h + 1)]
+
         def load_list(name, src):
             t = sbuf(name, [P, N // 16], U16)
             nc.sync.dma_start(t[:], src)
@@ -48,27 +60,27 @@ def tile_picked_yfoodwb_rel_po_kernel(
             queue.dma_start(t[:], src.bitcast(I32))
             return t
 
-        def scale_tile(engine, name, width):
+        def scale_tile(name, width):
             t = sbuf(name, [P, width], U8, tag=name)
-            engine.memset(t[:].bitcast(I32), 0)
+            nc.vector.memset(t[:].bitcast(I32), 0)
             return t
 
         def load_scales(queue, t, src, quadrants=range(4)):
             for q in quadrants:
                 queue.dma_start(t[32 * q : 32 * q + 4, :].bitcast(I32), src[0, 4 * q : 4 * q + 4, :].bitcast(I32))
 
-        def deal(name, words, scales):
-            dw = sbuf(name + "_words", [P, 2 * N], U8)
-            ds = sbuf(name + "_scales", [P, N], U8)
+        def deal(name, words, scales, tag=""):
+            dealt_words = sbuf(name + "_words", [P, 2 * N], U8, tag=tag)
+            dealt_scales = sbuf(name + "_scales", [P, N], U8)
             nc.vector.tensor_copy(
-                dw[:].bitcast(I32).rearrange("p (r b c) -> p b r c", r=4, c=4),
+                dealt_words[:].bitcast(I32).rearrange("p (r b c) -> p b r c", r=4, c=4),
                 words[:].rearrange("p (b r c) -> p b r c", r=4, c=4),
             )
             nc.vector.tensor_copy(
-                ds[:].bitcast(I32).rearrange("p (r b c) -> p b r c", r=4, c=2),
+                dealt_scales[:].bitcast(I32).rearrange("p (r b c) -> p b r c", r=4, c=2),
                 scales[:].bitcast(I32).rearrange("p (b r c) -> p b r c", r=4, c=2),
             )
-            return dw, ds
+            return dealt_words, dealt_scales
 
         def weight_pass(out, w, r, codes, scales, cols):
             nc.tensor.matmul_mx(
@@ -81,39 +93,40 @@ def tile_picked_yfoodwb_rel_po_kernel(
                 stop=True,
             )
 
-        def half_list(t, h):
-            return t[:, 16 * h : 16 * (h + 1)]
+        def quantise(codes, scales, values):
+            nc.vector.quantize_mx(out=codes.bitcast(FP8X4), scales=scales, in_=values)
 
-        xs_raw = scale_tile(nc.vector, "xs_raw", n_x)
-        w1s_raw = scale_tile(nc.vector, "w1s_raw", N)
-        es_raw = scale_tile(nc.vector, "es_raw", n_e)
-        w3s_raw = scale_tile(nc.vector, "w3s_raw", N)
-        w2s_raw = scale_tile(nc.vector, "w2s_raw", N)
-        w1w_raw = load_words(nc.gpsimd, "w1w_raw", w1_words[0])
+        xs_raw = scale_tile("xs_raw", predators)
+        w1s_raw = scale_tile("w1s_raw", N)
+        es_raw = scale_tile("es_raw", all_prey)
+        w3s_raw = scale_tile("w3s_raw", N)
+        w2s_raw = scale_tile("w2s_raw", N)
         unit_rows = sbuf("unit_rows", [P, P], F32)
+        ident = sbuf("ident", [P, P], F32)
+        abd_t = sbuf("abd_t", [P, all_prey], F32)
+
+        w1w_raw = load_words(nc.gpsimd, "w1w_raw", w1_words[0])
+        load_scales(nc.gpsimd, es_raw, e_scales, [3])
         nc.gpsimd.memset(unit_rows[:], 0.0)
-        for j, u in enumerate((unit, unit2)):
+        for j, factors in enumerate((unit, unit2)):
             nc.gpsimd.dma_start(
                 unit_rows[4 * j : 4 * j + 4, :].rearrange("r (b q) -> r b q", q=8),
-                u.rearrange("(b r q) o -> r b (q o)", r=4, q=8),
+                factors.rearrange("(b r q) o -> r b (q o)", r=4, q=8),
             )
-        ident = sbuf("ident", [P, P], F32)
         make_identity(nc, ident[:])
 
         offs_t = load_list("offs_t", offs)
         xw_raw = load_words(nc.sync, "xw_raw", x_words[0].rearrange("p n t -> p (n t)"))
         load_scales(nc.sync, xs_raw, x_scales)
         pry_t = load_list("pry_t", pry)
-        load_scales(nc.sync, es_raw, e_scales, range(1))
         ew_raw = load_words(nc.sync, "ew_raw", e_words[0].rearrange("p n t -> p (n t)"))
         load_scales(nc.sync, w1s_raw, w1_scales)
-        load_scales(nc.sync, es_raw, e_scales, range(1, 4))
+        load_scales(nc.sync, es_raw, e_scales, range(3))
         w3w_raw = load_words(nc.sync, "w3w_raw", w3_words[0])
         load_scales(nc.sync, w3s_raw, w3_scales)
         w2w_raw = load_words(nc.sync, "w2w_raw", w2_words[0])
         ref_t = load_list("ref_t", ref)
         load_scales(nc.sync, w2s_raw, w2_scales)
-        abd_t = sbuf("abd_t", [P, n_e], F32)
         nc.sync.dma_start(abd_t[:], abd)
         sw_t = load_list("sw_t", sw)
 
@@ -121,7 +134,7 @@ def tile_picked_yfoodwb_rel_po_kernel(
         xs = sbuf("xs", [P, N], U8)
         nc.vector.tensor_copy(xw[:], xw_raw[:].bitcast(U32).indirect(offs_t[:]))
         nc.vector.tensor_copy(xs[:], xs_raw[:].indirect(offs_t[:]))
-        w1 = deal("w1", w1w_raw, w1s_raw)
+        w1 = deal("w1", w1w_raw, w1s_raw, tag="xs_raw")
         ew = sbuf("ew", [P, N], U32, tag="w1s_raw")
         es = sbuf("es", [P, N], U8)
         nc.vector.tensor_copy(ew[:], ew_raw[:].bitcast(U32).indirect(pry_t[:]))
@@ -141,72 +154,77 @@ def tile_picked_yfoodwb_rel_po_kernel(
             )
         units_ps = bank(0, "units_ps")
         nc.tensor.transpose(units_ps[:, 0:P], unit_rows[:], ident[:])
-        units = sbuf("units", [P, 8], F32)
+        units = sbuf("units", [P, 8], F32, tag="w3s_raw")
         nc.vector.tensor_copy(units[:], units_ps[:, 0:8])
 
-        th = []
+        refuge = [sbuf("refuge%d" % r, [P, N], F32) for r in range(4)]
         for r in range(4):
             yg = bank(4 + r, "yg%d" % r)
             weight_pass(yg[:], w3, r, ew, es, slice(0, N))
-            t = sbuf("th%d" % r, [P, N], F32)
-            nc.scalar.activation(t[:], yg[:], ACT.Tanh, scale=0.5)
-            th.append(t)
+            nc.scalar.activation(refuge[r][:], yg[:], ACT.Tanh, scale=0.5)
         ye = {}
         for h in range(2):
             for pair in range(2):
-                t = bank(2 * h + pair, "ye%d_%d" % (h, pair))
+                both = bank(2 * h + pair, "ye%d_%d" % (h, pair))
                 for j in range(2):
-                    ye[h, 2 * pair + j] = t[:, HALF * j : HALF * (j + 1)]
-                    weight_pass(ye[h, 2 * pair + j], w2, 2 * pair + j, ew, es, slice(HALF * h, HALF * (h + 1)))
+                    ye[h, 2 * pair + j] = both[:, half(j)]
+                    weight_pass(ye[h, 2 * pair + j], w2, 2 * pair + j, ew, es, half(h))
 
-        hid = sbuf("hid", [P, N, 4], BF16, tag="w3s_raw")
+        hid = sbuf("hid", [P, 4, P, 4], BF16)
         nc.vector.tensor_tensor(
             hid[:],
-            att[:].rearrange("p s b m r -> p (s b m) r"),
-            units[:, 0:4].rearrange("p (o r) -> p o r", o=1).to_broadcast([P, N, 4]),
+            att[:].rearrange("p s b m r -> p s (b m) r"),
+            units[:, 0:4].rearrange("p (s m r) -> p s m r", s=1, m=1).to_broadcast([P, 4, P, 4]),
             ALU.mult,
         )
+        levelled = sbuf("levelled", [P, N], F32)
+        nc.vector.tensor_scalar(levelled[:], refuge[VECTOR_GATE[1]][:], GATE_SLOPE, GATE_LEVEL, ALU.mult, ALU.add)
         hid_codes = sbuf("hid_codes", [P, N], U32)
         hid_scales = sbuf("hid_scales", [P, N], U8)
-        nc.vector.quantize_mx(out=hid_codes[:].bitcast(FP8X4), scales=hid_scales[:], in_=hid[:].rearrange("p n r -> p (n r)"))
+        quantise(hid_codes[:], hid_scales[:], hid[:].rearrange("p s n r -> p (s n r)"))
 
         scores = {}
         top = sbuf("top", [P, 4, N], F32)
         sums = sbuf("sums", [P, 4, 2], F32)
+        total = sbuf("total", [P, 4], F32)
+        shift = sbuf("shift", [P, 4], F32)
         for h in range(2):
-            cols = slice(HALF * h, HALF * (h + 1))
             planes = sbuf("planes%d" % h, [P, 4, HALF], BF16, tag="planes")
             for r in range(4):
                 gate = sbuf("gate%d_%d" % (h, r), [P, HALF], F32)
-                nc.scalar.activation(gate[:], th[r][:].indirect(half_list(ref_t, h)), ACT.Copy, scale=-0.35, bias=0.85)
-                nc.vector.scalar_tensor_tensor(planes[:, r, :], ye[h, r], units[:, 4 + r : 5 + r], gate[:], ALU.mult, ALU.mult)
+                if (h, r) == VECTOR_GATE:
+                    nc.vector.tensor_copy(gate[:], levelled[:].indirect(half_list(ref_t, h)))
+                else:
+                    fetched_refuge = refuge[r][:].indirect(half_list(ref_t, h))
+                    nc.scalar.activation(gate[:], fetched_refuge, ACT.Copy, scale=GATE_SLOPE, bias=GATE_LEVEL)
+                nc.vector.scalar_tensor_tensor(
+                    planes[:, r, :], ye[h, r], units[:, 4 + r : 5 + r], gate[:], ALU.mult, ALU.mult
+                )
             hid2 = sbuf("hid2_%d" % h, [P, HALF, 4], BF16, tag="hid2_%d" % h)
             nc.vector.tensor_copy(hid2[:], planes[:].rearrange("p r n -> p n r"))
-            codes = sbuf("hid2_codes%d" % h, [P, HALF], U32)
-            scales = sbuf("hid2_scales%d" % h, [P, HALF], U8)
-            nc.vector.quantize_mx(out=codes[:].bitcast(FP8X4), scales=scales[:], in_=hid2[:].rearrange("p n r -> p (n r)"))
+            hid2_codes = sbuf("hid2_codes%d" % h, [P, HALF], U32)
+            hid2_scales = sbuf("hid2_scales%d" % h, [P, HALF], U8)
+            quantise(hid2_codes[:], hid2_scales[:], hid2[:].rearrange("p n r -> p (n r)"))
             for pair in range(2):
-                sc = bank(4 + 2 * h + pair, "sc%d_%d" % (h, pair))
+                scores[h, pair] = bank(4 + 2 * h + pair, "sc%d_%d" % (h, pair))
                 for j in range(2):
                     s = 2 * pair + j
                     nc.tensor.matmul_mx(
-                        out=sc[:, HALF * j : HALF * (j + 1)],
+                        out=scores[h, pair][:, half(j)],
                         lhsT=hid_codes[:, P * s : P * (s + 1)].bitcast(FP8X4),
                         lhsT_scale=hid_scales[:, P * s : P * (s + 1)],
-                        rhs=codes[:].bitcast(FP8X4),
-                        rhs_scale=scales[:],
+                        rhs=hid2_codes[:].bitcast(FP8X4),
+                        rhs_scale=hid2_scales[:],
                         start=True,
                         stop=True,
                     )
-                scores[h, pair] = sc
 
-        prey = sbuf("prey", [P, N], F32)
-        nc.scalar.activation(prey[:], abd_t[:].indirect(pry_t[:]), ACT.Copy)
-        rate = sbuf("rate", [P, 4, N], F32, tag="hid2_1")
-
+        prey = sbuf("prey", [P, N], F32, tag="hid2_1")
+        nc.vector.tensor_copy(prey[:], abd_t[:].indirect(pry_t[:]))
+        rate = sbuf("rate", [P, 4, N], F32)
         for h in range(2):
-            cols = slice(HALF * h, HALF * (h + 1))
             for pair in range(2):
+                two = slice(2 * pair, 2 * pair + 2)
                 bounded = sbuf("bounded%d_%d" % (h, pair), [P, N], F32)
                 nc.scalar.activation(bounded[:], scores[h, pair][:], ACT.Tanh)
                 growth = sbuf("growth%d_%d" % (h, pair), [P, 2, HALF], F32)
@@ -214,47 +232,56 @@ def tile_picked_yfoodwb_rel_po_kernel(
                 for j in range(2):
                     s = 2 * pair + j
                     nc.vector.scalar_tensor_tensor(
-                        rate[:, s, cols], growth[:, j, :], 1.0, prey[:, cols], ALU.mult, ALU.mult, accum_out=sums[:, s, h : h + 1]
+                        rate[:, s, half(h)], growth[:, j, :], 1.0, prey[:, half(h)], ALU.mult, ALU.mult,
+                        accum_out=sums[:, s, h : h + 1],
                     )
-
-        total = sbuf("total", [P, 4], F32)
-        shift = sbuf("shift", [P, 4], F32)
-        for pair in range(2):
-            two = slice(2 * pair, 2 * pair + 2)
-            nc.vector.tensor_tensor(total[:, two], sums[:, two, 0], sums[:, two, 1], ALU.add)
-            nc.vector.tensor_scalar(shift[:, two], total[:, two], 0.5 / N, 0.25, ALU.mult, ALU.add)
+                if h == 1:
+                    nc.vector.tensor_tensor(total[:, two], sums[:, two, 0], sums[:, two, 1], ALU.add)
+                    nc.vector.tensor_scalar(shift[:, two], total[:, two], 0.5 / N, 0.25, ALU.mult, ALU.add)
+            for pair in range(2):
+                two = slice(2 * pair, 2 * pair + 2)
+                nc.vector.tensor_tensor(
+                    top[:, two, half(h)],
+                    rate[:, two, half(h)],
+                    prey[:, half(h)].rearrange("p (o n) -> p o n", o=1).to_broadcast([P, 2, HALF]),
+                    ALU.mult,
+                )
 
         inverse = []
         for s in range(4):
-            nc.vector.tensor_tensor(top[:, s, :], rate[:, s, :], prey[:], ALU.mult)
-            root = sbuf("root%d" % s, [P, N], F32)
+            root = sbuf("root%d" % s, [P, N], F32, tag="root%d" % s)
             nc.scalar.activation(root[:], rate[:, s, :], ACT.Abs_reciprocal_sqrt, bias=shift[:, s : s + 1])
-            size = sbuf("size%d" % s, [P, N], F32)
-            nc.scalar.activation(size[:], root[:], ACT.Square)
-            sign = sbuf("sign%d" % s, [P, N], F32)
-            nc.scalar.activation(sign[:], rate[:, s, :], ACT.Sign, bias=shift[:, s : s + 1])
-            inv = sbuf("inverse%d" % s, [P, N], F32)
-            nc.vector.tensor_tensor(inv[:], sign[:], size[:], ALU.mult)
-            inverse.append(inv)
+            size = sbuf("size%d" % s, [P, N], F32, tag="size%d" % s)
+            nc.scalar.activation(size[:], root[:], ACT.Square, scale=math.sqrt(2.0))
+            positive = sbuf("positive%d" % s, [P, N], F32)
+            inverse.append(sbuf("inverse%d" % s, [P, N], F32))
+            nc.vector.tensor_scalar(positive[:], rate[:, s, :], shift[:, s : s + 1], 0.0, ALU.add, ALU.is_gt)
+            nc.vector.scalar_tensor_tensor(inverse[s][:], positive[:], 0.5, size[:], ALU.subtract, ALU.mult)
 
         out_rows = out_0.rearrange("(p s) e -> p s e", s=4)
         out_words = out_1[0].rearrange("p n t -> p (n t)").bitcast(I32)
         out_scales = sbuf("out_scales", [P, N], U8)
         for h in range(2):
-            cols = slice(HALF * h, HALF * (h + 1))
-            result = sbuf("result%d" % h, [P, 4, HALF], F32)
+            result = sbuf("result%d" % h, [P, 4, HALF], F32, tag="size3" if h else "")
             for s in range(4):
-                nc.vector.tensor_tensor(result[:, s, :], inverse[s][:].indirect(half_list(sw_t, h)), top[:, s, cols], ALU.mult)
-            nc.sync.dma_start(out_rows[:, :, cols], result[:])
+                looked_up = inverse[s][:].indirect(half_list(sw_t, h))
+                if h == 1 and s < SCALAR_SLOTS:
+                    fetched = sbuf("fetched%d" % s, [P, HALF], F32, tag="" if s else "root3")
+                    nc.scalar.activation(fetched[:], looked_up, ACT.Copy)
+                    looked_up = fetched[:]
+                nc.vector.tensor_tensor(result[:, s, :], looked_up, top[:, s, half(h)], ALU.mult)
+                if s % 2:
+                    nc.sync.dma_start(out_rows[:, s - 1 : s + 1, half(h)], result[:, s - 1 : s + 1, :])
             rounded = sbuf("rounded%d" % h, [P, HALF, 4], BF16)
             turned = result[:].rearrange("p s n -> p n s")
             if h == 0:
                 nc.scalar.copy(rounded[:], turned)
             else:
-                nc.vector.tensor_copy(rounded[:], turned)
+                nc.scalar.copy(rounded[:, 0:SCALAR_COLUMNS, :], turned[:, 0:SCALAR_COLUMNS, :])
+                nc.vector.tensor_copy(rounded[:, SCALAR_COLUMNS:HALF, :], turned[:, SCALAR_COLUMNS:HALF, :])
             out_codes = sbuf("out_codes%d" % h, [P, HALF], U32)
-            nc.vector.quantize_mx(out=out_codes[:].bitcast(FP8X4), scales=out_scales[:, cols], in_=rounded[:].rearrange("p n s -> p (n s)"))
-            nc.sync.dma_start(out_words[:, cols], out_codes[:].bitcast(I32))
+            quantise(out_codes[:], out_scales[:, half(h)], rounded[:].rearrange("p n s -> p (n s)"))
+            nc.sync.dma_start(out_words[:, half(h)], out_codes[:].bitcast(I32))
         for q in range(4):
             queue = nc.scalar if q % 2 else nc.sync
             queue.dma_start(out_2[0, 4 * q : 4 * q + 4, :].bitcast(I32), out_scales[32 * q : 32 * q + 4, :].bitcast(I32))

@@ -21,7 +21,7 @@ HALF = N // 2
 FLOPS = 4 * 2 * N * N * N
 
 GATE_SLOPE, GATE_LEVEL = -0.35, 0.85
-VECTOR_GATE = (0, 3)
+VECTOR_PLANE = 0
 SCALAR_SLOTS = 2
 SCALAR_COLUMNS = 96
 
@@ -73,12 +73,12 @@ def tile_picked_yfoodwb_rel_po_kernel(
             dealt_words = sbuf(name + "_words", [P, 2 * N], U8, tag=tag)
             dealt_scales = sbuf(name + "_scales", [P, N], U8)
             nc.vector.tensor_copy(
-                dealt_words[:].bitcast(I32).rearrange("p (r b c) -> p b r c", r=4, c=4),
-                words[:].rearrange("p (b r c) -> p b r c", r=4, c=4),
+                dealt_words[:].bitcast(I32).rearrange("p (r b c) -> p r b c", r=4, c=4),
+                words[:].rearrange("p (b r c) -> p r b c", r=4, c=4),
             )
             nc.vector.tensor_copy(
-                dealt_scales[:].bitcast(I32).rearrange("p (r b c) -> p b r c", r=4, c=2),
-                scales[:].bitcast(I32).rearrange("p (b r c) -> p b r c", r=4, c=2),
+                dealt_scales[:].bitcast(I32).rearrange("p (r b c) -> p r b c", r=4, c=2),
+                scales[:].bitcast(I32).rearrange("p (b r c) -> p r b c", r=4, c=2),
             )
             return dealt_words, dealt_scales
 
@@ -91,6 +91,11 @@ def tile_picked_yfoodwb_rel_po_kernel(
                 rhs_scale=scales[:, cols],
                 start=True,
                 stop=True,
+            )
+
+        def side_by_side(out, rows):
+            nc.vector.tensor_copy(
+                out.rearrange("p (c i) j -> p c j i", i=4), rows.rearrange("p j (c i) -> p c j i", i=4)
             )
 
         def quantise(codes, scales, values):
@@ -170,7 +175,7 @@ def tile_picked_yfoodwb_rel_po_kernel(
                     ye[h, 2 * pair + j] = both[:, half(j)]
                     weight_pass(ye[h, 2 * pair + j], w2, 2 * pair + j, ew, es, half(h))
 
-        hid = sbuf("hid", [P, 4, P, 4], BF16)
+        hid = sbuf("hid", [P, 4, P, 4], BF16, tag="w2w_raw")
         nc.vector.tensor_tensor(
             hid[:],
             att[:].rearrange("p s b m r -> p s (b m) r"),
@@ -178,7 +183,7 @@ def tile_picked_yfoodwb_rel_po_kernel(
             ALU.mult,
         )
         levelled = sbuf("levelled", [P, N], F32)
-        nc.vector.tensor_scalar(levelled[:], refuge[VECTOR_GATE[1]][:], GATE_SLOPE, GATE_LEVEL, ALU.mult, ALU.add)
+        nc.vector.tensor_scalar(levelled[:], refuge[VECTOR_PLANE][:], GATE_SLOPE, GATE_LEVEL, ALU.mult, ALU.add)
         hid_codes = sbuf("hid_codes", [P, N], U32)
         hid_scales = sbuf("hid_scales", [P, N], U8)
         quantise(hid_codes[:], hid_scales[:], hid[:].rearrange("p s n r -> p (s n r)"))
@@ -186,13 +191,12 @@ def tile_picked_yfoodwb_rel_po_kernel(
         scores = {}
         top = sbuf("top", [P, 4, N], F32)
         sums = sbuf("sums", [P, 4, 2], F32)
-        total = sbuf("total", [P, 4], F32)
         shift = sbuf("shift", [P, 4], F32)
         for h in range(2):
             planes = sbuf("planes%d" % h, [P, 4, HALF], BF16, tag="planes")
             for r in range(4):
                 gate = sbuf("gate%d_%d" % (h, r), [P, HALF], F32)
-                if (h, r) == VECTOR_GATE:
+                if r == VECTOR_PLANE:
                     nc.vector.tensor_copy(gate[:], levelled[:].indirect(half_list(ref_t, h)))
                 else:
                     fetched_refuge = refuge[r][:].indirect(half_list(ref_t, h))
@@ -201,7 +205,7 @@ def tile_picked_yfoodwb_rel_po_kernel(
                     planes[:, r, :], ye[h, r], units[:, 4 + r : 5 + r], gate[:], ALU.mult, ALU.mult
                 )
             hid2 = sbuf("hid2_%d" % h, [P, HALF, 4], BF16, tag="hid2_%d" % h)
-            nc.vector.tensor_copy(hid2[:], planes[:].rearrange("p r n -> p n r"))
+            side_by_side(hid2[:], planes[:])
             hid2_codes = sbuf("hid2_codes%d" % h, [P, HALF], U32)
             hid2_scales = sbuf("hid2_scales%d" % h, [P, HALF], U8)
             quantise(hid2_codes[:], hid2_scales[:], hid2[:].rearrange("p n r -> p (n r)"))
@@ -236,8 +240,7 @@ def tile_picked_yfoodwb_rel_po_kernel(
                         accum_out=sums[:, s, h : h + 1],
                     )
                 if h == 1:
-                    nc.vector.tensor_tensor(total[:, two], sums[:, two, 0], sums[:, two, 1], ALU.add)
-                    nc.vector.tensor_scalar(shift[:, two], total[:, two], 0.5 / N, 0.25, ALU.mult, ALU.add)
+                    nc.vector.scalar_tensor_tensor(shift[:, two], sums[:, two, 0], N / 2, sums[:, two, 1], ALU.add, ALU.add)
             for pair in range(2):
                 two = slice(2 * pair, 2 * pair + 2)
                 nc.vector.tensor_tensor(
@@ -250,12 +253,12 @@ def tile_picked_yfoodwb_rel_po_kernel(
         inverse = []
         for s in range(4):
             root = sbuf("root%d" % s, [P, N], F32, tag="root%d" % s)
-            nc.scalar.activation(root[:], rate[:, s, :], ACT.Abs_reciprocal_sqrt, bias=shift[:, s : s + 1])
+            nc.scalar.activation(root[:], rate[:, s, :], ACT.Abs_reciprocal_sqrt, scale=2.0 * N, bias=shift[:, s : s + 1])
             size = sbuf("size%d" % s, [P, N], F32, tag="size%d" % s)
-            nc.scalar.activation(size[:], root[:], ACT.Square, scale=math.sqrt(2.0))
+            nc.scalar.activation(size[:], root[:], ACT.Square, scale=math.sqrt(4.0 * N))
             positive = sbuf("positive%d" % s, [P, N], F32)
             inverse.append(sbuf("inverse%d" % s, [P, N], F32))
-            nc.vector.tensor_scalar(positive[:], rate[:, s, :], shift[:, s : s + 1], 0.0, ALU.add, ALU.is_gt)
+            nc.vector.tensor_scalar(positive[:], rate[:, s, :], -2.0 * N, shift[:, s : s + 1], ALU.mult, ALU.is_lt)
             nc.vector.scalar_tensor_tensor(inverse[s][:], positive[:], 0.5, size[:], ALU.subtract, ALU.mult)
 
         out_rows = out_0.rearrange("(p s) e -> p s e", s=4)
@@ -278,7 +281,7 @@ def tile_picked_yfoodwb_rel_po_kernel(
                 nc.scalar.copy(rounded[:], turned)
             else:
                 nc.scalar.copy(rounded[:, 0:SCALAR_COLUMNS, :], turned[:, 0:SCALAR_COLUMNS, :])
-                nc.vector.tensor_copy(rounded[:, SCALAR_COLUMNS:HALF, :], turned[:, SCALAR_COLUMNS:HALF, :])
+                side_by_side(rounded[:, SCALAR_COLUMNS:HALF, :], result[:, :, SCALAR_COLUMNS:HALF])
             out_codes = sbuf("out_codes%d" % h, [P, HALF], U32)
             quantise(out_codes[:], out_scales[:, half(h)], rounded[:].rearrange("p n s -> p (n s)"))
             nc.sync.dma_start(out_words[:, half(h)], out_codes[:].bitcast(I32))

import math
from contextlib import ExitStack

import concourse.mybir as mybir
from concourse.masks import make_identity

F32 = mybir.dt.float32
BF16 = mybir.dt.bfloat16
I32 = mybir.dt.int32
U32 = mybir.dt.uint32
U16 = mybir.dt.uint16
U8 = mybir.dt.uint8
FP8X4 = mybir.dt.float8_e4m3fn_x4
FP4X4 = mybir.dt.float4_e2m1fn_x4
ALU = mybir.AluOpType
ACT = mybir.ActivationFunctionType

P = 128
N = 512
HALF = N // 2
FLOPS = 4 * 2 * N * N * N

GATE_SLOPE, GATE_LEVEL = -0.35, 0.85
VECTOR_PLANE = 0
SCALAR_SLOTS = 2
SCALAR_COLUMNS = 96


def tile_picked_yfoodwb_rel_po_kernel(
    tc, x_words, x_scales, w1_words, w1_scales, e_words, e_scales, w2_words, w2_scales,
    w3_words, w3_scales, unit, unit2, abd, offs, pry, ref, sw, out_0, out_1, out_2,
):
    nc = tc.nc
    predators = x_scales.shape[2]
    all_prey = e_scales.shape[2]

    with ExitStack() as ctx:
        sb = ctx.enter_context(tc.tile_pool(name="sb", bufs=1))
        psum = ctx.enter_context(tc.psum_pool(name="psum", bufs=1))

        def sbuf(name, shape, dtype, tag=""):
            return sb.tile(shape, dtype, name=name, tag=tag, align_bytes=64)

        def bank(i, name):
            return psum.tile([P, N], F32, name=name, tag="bank%d" % i)

        def half(h):
            return slice(HALF * h, HALF * (h + 1))

        def half_list(t, h):
            return t[:, 16 * h : 16 * (h + 1)]

        def load_list(name, src):
            t = sbuf(name, [P, N // 16], U16)
            nc.sync.dma_start(t[:], src)
            return t

        def load_words(queue, name, src):
            t = sbuf(name, [P, src.shape[1] // 4], I32, tag=name)
            queue.dma_start(t[:], src.bitcast(I32))
            return t

        def scale_tile(name, width):
            t = sbuf(name, [P, width], U8, tag=name)
            nc.vector.memset(t[:].bitcast(I32), 0)
            return t

        def load_scales(queue, t, src, quadrants=range(4)):
            for q in quadrants:
                queue.dma_start(t[32 * q : 32 * q + 4, :].bitcast(I32), src[0, 4 * q : 4 * q + 4, :].bitcast(I32))

        def deal(name, words, scales, tag=""):
            dealt_words = sbuf(name + "_words", [P, 2 * N], U8, tag=tag)
            dealt_scales = sbuf(name + "_scales", [P, N], U8)
            nc.vector.tensor_copy(
                dealt_words[:].bitcast(I32).rearrange("p (r b c) -> p r b c", r=4, c=4),
                words[:].rearrange("p (b r c) -> p r b c", r=4, c=4),
            )
            nc.vector.tensor_copy(
                dealt_scales[:].bitcast(I32).rearrange("p (r b c) -> p r b c", r=4, c=2),
                scales[:].bitcast(I32).rearrange("p (b r c) -> p r b c", r=4, c=2),
            )
            return dealt_words, dealt_scales

        def weight_pass(out, w, r, codes, scales, cols):
            nc.tensor.matmul_mx(
                out=out,
                lhsT=w[0][:, 2 * P * r : 2 * P * (r + 1)].bitcast(FP4X4),
                lhsT_scale=w[1][:, P * r : P * (r + 1)],
                rhs=codes[:, cols].bitcast(FP8X4),
                rhs_scale=scales[:, cols],
                start=True,
                stop=True,
            )

        def side_by_side(out, rows):
            nc.vector.tensor_copy(
                out.rearrange("p (c i) j -> p c j i", i=4), rows.rearrange("p j (c i) -> p c j i", i=4)
            )

        def quantise(codes, scales, values):
            nc.vector.quantize_mx(out=codes.bitcast(FP8X4), scales=scales, in_=values)

        xs_raw = scale_tile("xs_raw", predators)
        w1s_raw = scale_tile("w1s_raw", N)
        es_raw = scale_tile("es_raw", all_prey)
        w3s_raw = scale_tile("w3s_raw", N)
        w2s_raw = scale_tile("w2s_raw", N)
        unit_rows = sbuf("unit_rows", [P, P], F32)
        ident = sbuf("ident", [P, P], F32)
        abd_t = sbuf("abd_t", [P, all_prey], F32)

        w1w_raw = load_words(nc.gpsimd, "w1w_raw", w1_words[0])
        load_scales(nc.gpsimd, es_raw, e_scales, [3])
        nc.gpsimd.memset(unit_rows[:], 0.0)
        for j, factors in enumerate((unit, unit2)):
            nc.gpsimd.dma_start(
                unit_rows[4 * j : 4 * j + 4, :].rearrange("r (b q) -> r b q", q=8),
                factors.rearrange("(b r q) o -> r b (q o)", r=4, q=8),
            )
        make_identity(nc, ident[:])

        offs_t = load_list("offs_t", offs)
        xw_raw = load_words(nc.sync, "xw_raw", x_words[0].rearrange("p n t -> p (n t)"))
        load_scales(nc.sync, xs_raw, x_scales)
        pry_t = load_list("pry_t", pry)
        ew_raw = load_words(nc.sync, "ew_raw", e_words[0].rearrange("p n t -> p (n t)"))
        load_scales(nc.sync, w1s_raw, w1_scales)
        load_scales(nc.sync, es_raw, e_scales, range(3))
        w3w_raw = load_words(nc.sync, "w3w_raw", w3_words[0])
        load_scales(nc.sync, w3s_raw, w3_scales)
        w2w_raw = load_words(nc.sync, "w2w_raw", w2_words[0])
        ref_t = load_list("ref_t", ref)
        load_scales(nc.sync, w2s_raw, w2_scales)
        nc.sync.dma_start(abd_t[:], abd)
        sw_t = load_list("sw_t", sw)

        xw = sbuf("xw", [P, N], U32)
        xs = sbuf("xs", [P, N], U8)
        nc.vector.tensor_copy(xw[:], xw_raw[:].bitcast(U32).indirect(offs_t[:]))
        nc.vector.tensor_copy(xs[:], xs_raw[:].indirect(offs_t[:]))
        w1 = deal("w1", w1w_raw, w1s_raw, tag="xs_raw")
        ew = sbuf("ew", [P, N], U32, tag="w1s_raw")
        es = sbuf("es", [P, N], U8)
        nc.vector.tensor_copy(ew[:], ew_raw[:].bitcast(U32).indirect(pry_t[:]))
        nc.vector.tensor_copy(es[:], es_raw[:].indirect(pry_t[:]))
        w3 = deal("w3", w3w_raw, w3s_raw)
        w2 = deal("w2", w2w_raw, w2s_raw)

        att = sbuf("att", [P, 4, 4, 32, 4], F32)
        for b in range(4):
            y = bank(b, "y%d" % b)
            for r in range(4):
                weight_pass(y[:, P * r : P * (r + 1)], w1, r, xw, xs, slice(P * b, P * (b + 1)))
            nc.scalar.activation(
                att[:, :, b, :, :].rearrange("p s m r -> p m s r"),
                y[:].rearrange("p (r m s) -> p m s r", r=4, s=4),
                ACT.Gelu_apprx_tanh,
            )
        units_ps = bank(0, "units_ps")
        nc.tensor.transpose(units_ps[:, 0:P], unit_rows[:], ident[:])
        units = sbuf("units", [P, 8], F32, tag="w3s_raw")
        nc.vector.tensor_copy(units[:], units_ps[:, 0:8])

        refuge = [sbuf("refuge%d" % r, [P, N], F32) for r in range(4)]
        for r in range(4):
            yg = bank(4 + r, "yg%d" % r)
            weight_pass(yg[:], w3, r, ew, es, slice(0, N))
            nc.scalar.activation(refuge[r][:], yg[:], ACT.Tanh, scale=0.5)
        ye = {}
        for h in range(2):
            for pair in range(2):
                both = bank(2 * h + pair, "ye%d_%d" % (h, pair))
                for j in range(2):
                    ye[h, 2 * pair + j] = both[:, half(j)]
                    weight_pass(ye[h, 2 * pair + j], w2, 2 * pair + j, ew, es, half(h))

        hid = sbuf("hid", [P, 4, P, 4], BF16, tag="w2w_raw")
        nc.vector.tensor_tensor(
            hid[:],
            att[:].rearrange("p s b m r -> p s (b m) r"),
            units[:, 0:4].rearrange("p (s m r) -> p s m r", s=1, m=1).to_broadcast([P, 4, P, 4]),
            ALU.mult,
        )
        levelled = sbuf("levelled", [P, N], F32)
        nc.vector.tensor_scalar(levelled[:], refuge[VECTOR_PLANE][:], GATE_SLOPE, GATE_LEVEL, ALU.mult, ALU.add)
        hid_codes = sbuf("hid_codes", [P, N], U32)
        hid_scales = sbuf("hid_scales", [P, N], U8)
        quantise(hid_codes[:], hid_scales[:], hid[:].rearrange("p s n r -> p (s n r)"))

        scores = {}
        top = sbuf("top", [P, 4, N], F32)
        sums = sbuf("sums", [P, 4, 2], F32)
        shift = sbuf("shift", [P, 4], F32)
        for h in range(2):
            planes = sbuf("planes%d" % h, [P, 4, HALF], BF16, tag="planes")
            for r in range(4):
                gate = sbuf("gate%d_%d" % (h, r), [P, HALF], F32)
                if r == VECTOR_PLANE:
                    nc.vector.tensor_copy(gate[:], levelled[:].indirect(half_list(ref_t, h)))
                else:
                    fetched_refuge = refuge[r][:].indirect(half_list(ref_t, h))
                    nc.scalar.activation(gate[:], fetched_refuge, ACT.Copy, scale=GATE_SLOPE, bias=GATE_LEVEL)
                nc.vector.scalar_tensor_tensor(
                    planes[:, r, :], ye[h, r], units[:, 4 + r : 5 + r], gate[:], ALU.mult, ALU.mult
                )
            hid2 = sbuf("hid2_%d" % h, [P, HALF, 4], BF16, tag="hid2_%d" % h)
            side_by_side(hid2[:], planes[:])
            hid2_codes = sbuf("hid2_codes%d" % h, [P, HALF], U32)
            hid2_scales = sbuf("hid2_scales%d" % h, [P, HALF], U8)
            quantise(hid2_codes[:], hid2_scales[:], hid2[:].rearrange("p n r -> p (n r)"))
            for pair in range(2):
                scores[h, pair] = bank(4 + 2 * h + pair, "sc%d_%d" % (h, pair))
                for j in range(2):
                    s = 2 * pair + j
                    nc.tensor.matmul_mx(
                        out=scores[h, pair][:, half(j)],
                        lhsT=hid_codes[:, P * s : P * (s + 1)].bitcast(FP8X4),
                        lhsT_scale=hid_scales[:, P * s : P * (s + 1)],
                        rhs=hid2_codes[:].bitcast(FP8X4),
                        rhs_scale=hid2_scales[:],
                        start=True,
                        stop=True,
                    )

        prey = sbuf("prey", [P, N], F32, tag="hid2_1")
        nc.vector.tensor_copy(prey[:], abd_t[:].indirect(pry_t[:]))
        rate = sbuf("rate", [P, 4, N], F32)
        for h in range(2):
            for pair in range(2):
                two = slice(2 * pair, 2 * pair + 2)
                bounded = sbuf("bounded%d_%d" % (h, pair), [P, N], F32)
                nc.scalar.activation(bounded[:], scores[h, pair][:], ACT.Tanh)
                growth = sbuf("growth%d_%d" % (h, pair), [P, 2, HALF], F32)
                nc.scalar.activation(growth[:].rearrange("p j n -> p (j n)"), bounded[:], ACT.Exp, scale=1.2)
                for j in range(2):
                    s = 2 * pair + j
                    nc.vector.scalar_tensor_tensor(
                        rate[:, s, half(h)], growth[:, j, :], 1.0, prey[:, half(h)], ALU.mult, ALU.mult,
                        accum_out=sums[:, s, h : h + 1],
                    )
                if h == 1:
                    nc.vector.scalar_tensor_tensor(shift[:, two], sums[:, two, 0], N / 2, sums[:, two, 1], ALU.add, ALU.add)
            for pair in range(2):
                two = slice(2 * pair, 2 * pair + 2)
                nc.vector.tensor_tensor(
                    top[:, two, half(h)],
                    rate[:, two, half(h)],
                    prey[:, half(h)].rearrange("p (o n) -> p o n", o=1).to_broadcast([P, 2, HALF]),
                    ALU.mult,
                )

        inverse = []
        for s in range(4):
            root = sbuf("root%d" % s, [P, N], F32, tag="root%d" % s)
            nc.scalar.activation(root[:], rate[:, s, :], ACT.Abs_reciprocal_sqrt, scale=2.0 * N, bias=shift[:, s : s + 1])
            size = sbuf("size%d" % s, [P, N], F32, tag="size%d" % s)
            nc.scalar.activation(size[:], root[:], ACT.Square, scale=math.sqrt(4.0 * N))
            positive = sbuf("positive%d" % s, [P, N], F32)
            inverse.append(sbuf("inverse%d" % s, [P, N], F32))
            nc.vector.tensor_scalar(positive[:], rate[:, s, :], -2.0 * N, shift[:, s : s + 1], ALU.mult, ALU.is_lt)
            nc.vector.scalar_tensor_tensor(inverse[s][:], positive[:], 0.5, size[:], ALU.subtract, ALU.mult)

        out_rows = out_0.rearrange("(p s) e -> p s e", s=4)
        out_words = out_1[0].rearrange("p n t -> p (n t)").bitcast(I32)
        out_scales = sbuf("out_scales", [P, N], U8)
        for h in range(2):
            result = sbuf("result%d" % h, [P, 4, HALF], F32, tag="size3" if h else "")
            for s in range(4):
                looked_up = inverse[s][:].indirect(half_list(sw_t, h))
                if h == 1 and s < SCALAR_SLOTS:
                    fetched = sbuf("fetched%d" % s, [P, HALF], F32, tag="" if s else "root3")
                    nc.scalar.activation(fetched[:], looked_up, ACT.Copy)
                    looked_up = fetched[:]
                nc.vector.tensor_tensor(result[:, s, :], looked_up, top[:, s, half(h)], ALU.mult)
                if s % 2:
                    nc.sync.dma_start(out_rows[:, s - 1 : s + 1, half(h)], result[:, s - 1 : s + 1, :])
            rounded = sbuf("rounded%d" % h, [P, HALF, 4], BF16)
            turned = result[:].rearrange("p s n -> p n s")
            if h == 0:
                nc.scalar.copy(rounded[:], turned)
            else:
                nc.scalar.copy(rounded[:, 0:SCALAR_COLUMNS, :], turned[:, 0:SCALAR_COLUMNS, :])
                side_by_side(rounded[:, SCALAR_COLUMNS:HALF, :], result[:, :, SCALAR_COLUMNS:HALF])
            out_codes = sbuf("out_codes%d" % h, [P, HALF], U32)
            quantise(out_codes[:], out_scales[:, half(h)], rounded[:].rearrange("p n s -> p (n s)"))
            nc.sync.dma_start(out_words[:, half(h)], out_codes[:].bitcast(I32))
        for q in range(4):
            queue = nc.scalar if q % 2 else nc.sync
            queue.dma_start(out_2[0, 4 * q : 4 * q + 4, :].bitcast(I32), out_scales[32 * q : 32 * q + 4, :].bitcast(I32))
